import numpy as np
import ml_dtypes


def mxq(x, axis, fmt="e4m3"):
    dtype, down = {"e4m3": (ml_dtypes.float8_e4m3fn, 7), "e5m2": (ml_dtypes.float8_e5m2, 14)}[fmt]
    v = np.moveaxis(np.asarray(x, np.float32).astype(ml_dtypes.bfloat16).astype(np.float64), axis, -1)
    blocks = v.reshape(v.shape[:-1] + (-1, 32))
    amax = np.abs(blocks).max(-1, keepdims=True)
    byte = np.maximum(np.where(amax > 0, np.frexp(amax)[1] - 1 + 127, 0) - down, 1)
    scale = np.exp2(byte - 127.0)
    codes = (blocks / scale).astype(np.float32).astype(dtype).astype(np.float64)
    return np.moveaxis((codes * scale).reshape(v.shape), -1, axis)


WIDE = False


def mx_kscale(k):
    if not WIDE:
        return np.ones(k)
    levels = np.array([10, -10, 5, -5, 0])
    if k % 512:
        return np.exp2(np.random.permutation(np.resize(levels, k // 32))).repeat(32)
    a = np.empty((k // 512, 16))
    for p in range(k // 512):
        a[p, :8] = np.random.permutation(np.resize(levels, 8))
        for g in range(8):
            far = levels[np.abs(levels - a[p, g]) >= 10]
            a[p, g + 8] = far[np.random.randint(len(far))]
    return np.exp2(a.ravel()).repeat(32)


def f64(x):
    return np.asarray(x).astype(np.float64)


E2M1 = np.array([0.0, 0.5, 1.0, 1.5, 2.0, 3.0, 4.0, 6.0, -0.0, -0.5, -1.0, -1.5, -2.0, -3.0, -4.0, -6.0])


def pack_weight(w, fmt):
    k, n = w.shape
    w = f64(np.asarray(w, np.float32).astype(ml_dtypes.bfloat16)).reshape(k // 32, 32, n)
    amax = np.abs(w).max(1)
    if fmt == "e4m3":
        byte = np.frexp(amax)[1] - 1 + 127 - 7
    else:
        mant, ex = np.frexp(amax / 6.0)
        byte = np.where(mant > 0.5, ex, ex - 1) + 127
    byte = np.clip(np.where(amax > 0, byte, 1), 1, 254)
    scaled = (w * np.exp2(127.0 - byte)[:, None, :]).reshape(k, n).astype(np.float32)
    by_word = np.ascontiguousarray(scaled.reshape(k // 512, 128, 4, n).transpose(0, 1, 3, 2))
    if fmt == "e4m3":
        words = by_word.astype(ml_dtypes.float8_e4m3fn).view(np.uint8)
    else:
        c = by_word.astype(ml_dtypes.float4_e2m1fn).view(np.uint8) & 0xF
        words = (c[..., 0::2] | (c[..., 1::2] << 4)).reshape(k // 512, 128, 2 * n)
    return np.ascontiguousarray(words), np.ascontiguousarray(byte.astype(np.uint8).reshape(k // 512, 16, n))


def unpack_weight(words, scales, fmt):
    g, _, n = scales.shape
    words = np.ascontiguousarray(words).reshape(g, 128, n, -1)
    if fmt == "e4m3":
        vals = words.view(ml_dtypes.float8_e4m3fn).astype(np.float64)
    else:
        nib = np.empty((g, 128, n, 4), np.uint8)
        nib[..., 0::2] = words & 0xF
        nib[..., 1::2] = words >> 4
        vals = E2M1[nib]
    vals = vals * np.repeat(np.exp2(scales.astype(np.float64) - 127.0), 8, axis=1)[..., None]
    return vals.transpose(0, 1, 3, 2).reshape(g * 512, n)


K, L, T, R, N, B = 512, 512, 1024, 512, 512, 512


def setup_inputs():
    n = np.random.standard_normal
    fk = mx_kscale(K)
    fr = mx_kscale(R)
    fl = mx_kscale(L)
    xtp = pack_weight(n((K, T)) / fk[:, None], "e4m3")
    wap = pack_weight(n((K, R)) * 1 / np.sqrt(K) * fk[:, None] * fr, "e2m1")
    xqp = pack_weight(n((L, T)) / fl[:, None], "e4m3")
    wcp = pack_weight(n((L, R)) * 1 / np.sqrt(L) * fl[:, None] * fr, "e2m1")
    wbp = pack_weight(n((R, N)) * 1 / np.sqrt(R) / fr[:, None], "e4m3")
    wyp = pack_weight(n((K, N)) * 1 / np.sqrt(K) * fk[:, None], "e2m1")
    return {
        "xt_words": xtp[0],
        "xt_scales": xtp[1],
        "wa_words": wap[0],
        "wa_scales": wap[1],
        "xq_words": xqp[0],
        "xq_scales": xqp[1],
        "wc_words": wcp[0],
        "wc_scales": wcp[1],
        "wb_words": wbp[0],
        "wb_scales": wbp[1],
        "wy_words": wyp[0],
        "wy_scales": wyp[1],
    }


def reference(xt_words, xt_scales, wa_words, wa_scales, xq_words, xq_scales, wc_words, wc_scales, wb_words, wb_scales, wy_words, wy_scales):
    xtu = unpack_weight(xt_words, xt_scales, "e4m3")
    wau = unpack_weight(wa_words, wa_scales, "e2m1")
    xqu = unpack_weight(xq_words, xq_scales, "e4m3")
    wcu = unpack_weight(wc_words, wc_scales, "e2m1")
    wbu = unpack_weight(wb_words, wb_scales, "e4m3")
    wyu = unpack_weight(wy_words, wy_scales, "e2m1")
    z = wau.T @ xtu + wcu.T @ xqu
    hid = z.reshape(R, B, T // B).max(axis=2)
    hidq = mxq(hid, 0, "e4m3")
    p = wbu.T @ hidq
    pr = np.repeat(p, T // B, axis=1)
    q = wyu.T @ xtu
    y = np.tanh(pr) + q
    return y

@@ -1,0 +1,194 @@
+from contextlib import ExitStack
+
+import concourse.mybir as mybir
+
+K, L, T, R, N, B = 512, 512, 1024, 512, 512, 512
+FLOPS = 2 * (K * R * T + L * R * T + R * N * B + K * N * T)
+
+F32 = mybir.dt.float32
+BF16 = mybir.dt.bfloat16
+I32 = mybir.dt.int32
+U32 = mybir.dt.uint32
+U16 = mybir.dt.uint16
+U8 = mybir.dt.uint8
+FP8X4 = mybir.dt.float8_e4m3fn_x4
+FP4X4 = mybir.dt.float4_e2m1fn_x4
+ALU = mybir.AluOpType
+
+P = 128
+PACK = 4
+BANK = 512
+STRIP = 128
+CHUNK = 256
+PAIRS = CHUNK // 2
+CHUNKS = T // CHUNK
+
+WA, WC, XT, XQ, WY, WB = 0, R, 2 * R, 2 * R + T, 2 * R + 2 * T, 2 * R + 2 * T + N
+PLANES = WB + N
+
+
+def tile_mix_hidden_peaks_of_pairs_kernel(
+    tc, xt_words, xt_scales, wa_words, wa_scales, xq_words, xq_scales,
+    wc_words, wc_scales, wb_words, wb_scales, wy_words, wy_scales, out,
+):
+    nc = tc.nc
+    with ExitStack() as ctx:
+        keep = ctx.enter_context(tc.tile_pool(name="keep", bufs=1))
+        work = ctx.enter_context(tc.tile_pool(name="work", bufs=CHUNKS))
+        psum = ctx.enter_context(tc.psum_pool(name="psum", bufs=1))
+        ctx.enter_context(tc.manual_schedule())
+
+        def load_words(name, words, bytes_a_column, first, last):
+            tile = keep.tile([P, (last - first) * bytes_a_column], U8, name=name, align_bytes=64)
+            nc.sync.dma_start(
+                out=tile[:].bitcast(I32),
+                in_=words[:, first * bytes_a_column : last * bytes_a_column].bitcast(I32),
+            )
+            return tile
+
+        xt_flat = xt_words[0].rearrange("p n t -> p (n t)")
+        xq_flat = xq_words[0].rearrange("p n t -> p (n t)")
+        wb_flat = wb_words[0].rearrange("p n t -> p (n t)")
+
+        planes = keep.tile([P, PLANES], U8, align_bytes=64)
+        nc.vector.memset(planes[:].bitcast(I32), 0)
+
+        landing = keep.tile([P, PLANES], U8, align_bytes=64)
+        for first, scales in ((WA, wa_scales), (WC, wc_scales), (XT, xt_scales),
+                              (XQ, xq_scales), (WY, wy_scales), (WB, wb_scales)):
+            width = scales.shape[2]
+            nc.sync.dma_start(
+                out=landing[4:P:8, first : first + width].bitcast(I32), in_=scales[0].bitcast(I32)
+            )
+        wa_raw = load_words("wa_raw", wa_words[0], 2, 0, R)
+        wc_raw = load_words("wc_raw", wc_words[0], 2, 0, R)
+        for r in range(4):
+            nc.sync.dma_start(
+                out=planes[r:P:32, :].bitcast(I32), in_=landing[4 + 8 * r : P : 32, :].bitcast(I32)
+            )
+        xt_head = load_words("xt_head", xt_flat, 4, 0, CHUNK)
+        xq_head = load_words("xq_head", xq_flat, 4, 0, CHUNK)
+        xt_rest = load_words("xt_rest", xt_flat, 4, CHUNK, T)
+        xq_rest = load_words("xq_rest", xq_flat, 4, CHUNK, T)
+        wy = load_words("wy", wy_words[0], 2, 0, N)
+        wb = load_words("wb", wb_flat, 4, 0, N)
+
+        def tokens(head, rest, first, count):
+            if first < CHUNK:
+                return head[:, 4 * first : 4 * (first + count)].bitcast(FP8X4)
+            return rest[:, 4 * (first - CHUNK) : 4 * (first - CHUNK + count)].bitcast(FP8X4)
+
+        first_layer = []
+        for name, raw, first in (("wa", wa_raw, WA), ("wc", wc_raw, WC)):
+            words = keep.tile([P, 2 * R], U8, name=name + "_words", align_bytes=64)
+            nc.scalar.copy(
+                out=words[:].bitcast(U16).rearrange("p (j m) -> p j m", j=PACK),
+                in_=raw[:].bitcast(U16).rearrange("p (m j) -> p j m", j=PACK),
+            )
+            plane = keep.tile([P, R], U8, name=name + "_plane", align_bytes=64)
+            nc.vector.tensor_copy(
+                out=plane[:].rearrange("p (j m) -> p j m", j=PACK),
+                in_=planes[:, first : first + R].rearrange("p (m j) -> p j m", j=PACK),
+            )
+            first_layer.append((words, plane))
+        inputs = ((xt_head, xt_rest, XT), (xq_head, xq_rest, XQ))
+
+        hidden, codes, code_planes, skips, squashed = {}, {}, {}, {}, {}
+
+        def peaks(c, s):
+            first = c * CHUNK + s * STRIP
+            strip = 2 * c + s
+            z = psum.tile([P, BANK], F32, name="z", tag="z%d" % (strip % 3))
+            for g in range(2):
+                words, plane = first_layer[g]
+                head, rest, x_plane = inputs[g]
+                for j in range(PACK):
+                    nc.tensor.matmul_mx(
+                        out=z[:, j * STRIP : (j + 1) * STRIP],
+                        lhsT=words[:, 2 * j * P : 2 * (j + 1) * P].bitcast(FP4X4),
+                        lhsT_scale=plane[:, j * P : (j + 1) * P],
+                        rhs=tokens(head, rest, first, STRIP),
+                        rhs_scale=planes[:, x_plane + first : x_plane + first + STRIP],
+                        start=(g == 0 and j == 0),
+                        stop=(g == 1 and j == PACK - 1),
+                    )
+            if s == 0:
+                hidden[c] = work.tile([P, PAIRS * PACK], BF16, name="hidden", align_bytes=64)
+            half = PAIRS * PACK // 2
+            peak = hidden[c][:, s * half : (s + 1) * half].rearrange("p (b j) -> p b j", j=PACK)
+            pairs = z[:].rearrange("p (j b e) -> p b j e", j=PACK, e=2)
+            odd = work.tile([P, STRIP // 2, PACK], F32, name="odd", tag="odd%d" % s)
+            nc.scalar.copy(out=odd[:], in_=pairs[:, :, :, 1])
+            nc.vector.tensor_tensor(out=peak, in0=pairs[:, :, :, 0], in1=odd[:], op=ALU.max)
+
+        def quantise(c):
+            codes[c] = work.tile([P, PAIRS], U32, name="codes", align_bytes=64)
+            code_planes[c] = work.tile([P, PAIRS], U8, name="code_plane", align_bytes=64)
+            nc.vector.quantize_mx(
+                out=codes[c][:].bitcast(FP8X4), scales=code_planes[c][:], in_=hidden[c][:]
+            )
+
+        def skip(c, h):
+            q = psum.tile([P, BANK], F32, name="q", tag="q%d" % (2 * (c % 2) + h))
+            for i in range(2):
+                rows = (2 * h + i) * P
+                nc.tensor.matmul_mx(
+                    out=q[:, i * CHUNK : (i + 1) * CHUNK],
+                    lhsT=wy[:, 2 * rows : 2 * (rows + P)].bitcast(FP4X4),
+                    lhsT_scale=planes[:, WY + rows : WY + rows + P],
+                    rhs=tokens(xt_head, xt_rest, c * CHUNK, CHUNK),
+                    rhs_scale=planes[:, XT + c * CHUNK : XT + (c + 1) * CHUNK],
+                    start=True,
+                    stop=True,
+                )
+            skips[c, h] = q
+
+        def second_layer(c):
+            p = psum.tile([P, BANK], F32, name="p", tag="p")
+            for i in range(N // P):
+                nc.tensor.matmul_mx(
+                    out=p[:, i * PAIRS : (i + 1) * PAIRS],
+                    lhsT=wb[:, 4 * i * P : 4 * (i + 1) * P].bitcast(FP8X4),
+                    lhsT_scale=planes[:, WB + i * P : WB + (i + 1) * P],
+                    rhs=codes[c][:].bitcast(FP8X4),
+                    rhs_scale=code_planes[c][:],
+                    start=True,
+                    stop=True,
+                )
+            for h in range(2):
+                th = work.tile([P, 2, PAIRS], F32, name="th", tag="th%d" % h)
+                nc.scalar.activation(
+                    out=th[:].rearrange("p i b -> p (i b)"),
+                    in_=p[:, 2 * h * PAIRS : 2 * (h + 1) * PAIRS],
+                    func=mybir.ActivationFunctionType.Tanh,
+                )
+                squashed[c, h] = th
+
+        out_rows = out.rearrange("(i p) t -> p i t", p=P)
+
+        def finish(c):
+            for h in range(2):
+                y = work.tile([P, 2, CHUNK], F32, name="y", tag="y%d" % h)
+                nc.vector.tensor_tensor(
+                    out=y[:].rearrange("p i (b e) -> p i b e", e=2),
+                    in0=skips[c, h][:].rearrange("p (i b e) -> p i b e", i=2, e=2),
+                    in1=squashed[c, h][:].unsqueeze(3).to_broadcast([P, 2, PAIRS, 2]),
+                    op=ALU.add,
+                )
+                nc.sync.dma_start(
+                    out=out_rows[:, 2 * h : 2 * h + 2, c * CHUNK : (c + 1) * CHUNK], in_=y[:]
+                )
+
+        def first_stage(c):
+            peaks(c, 0)
+            peaks(c, 1)
+            quantise(c)
+
+        first_stage(0)
+        for c in range(CHUNKS):
+            if c + 1 < CHUNKS:
+                first_stage(c + 1)
+            skip(c, 0)
+            second_layer(c)
+            skip(c, 1)
+            finish(c)

@@ -23,8 +23,11 @@ CHUNK = 256
 PAIRS = CHUNK // 2
 CHUNKS = T // CHUNK
 
-WA, WC, XT, XQ, WY, WB = 0, R, 2 * R, 2 * R + T, 2 * R + 2 * T, 2 * R + 2 * T + N
-PLANES = WB + N
+SIDE = R + T + N
+WA, XT, WY = 0, R, R + T
+WC, XQ, WB = SIDE + WA, SIDE + XT, SIDE + WY
+PLANES = 2 * SIDE
+EARLY = R + T // 2
 
 
 def tile_mix_hidden_peaks_of_pairs_kernel(
@@ -38,9 +41,9 @@ def tile_mix_hidden_peaks_of_pairs_kernel(
         psum = ctx.enter_context(tc.psum_pool(name="psum", bufs=1))
         ctx.enter_context(tc.manual_schedule())
 
-        def load_words(name, words, bytes_a_column, first, last):
+        def load_words(queue, name, words, bytes_a_column, first, last):
             tile = keep.tile([P, (last - first) * bytes_a_column], U8, name=name, align_bytes=64)
-            nc.sync.dma_start(
+            queue.dma_start(
                 out=tile[:].bitcast(I32),
                 in_=words[:, first * bytes_a_column : last * bytes_a_column].bitcast(I32),
             )
@@ -54,24 +57,37 @@ def tile_mix_hidden_peaks_of_pairs_kernel(
         nc.vector.memset(planes[:].bitcast(I32), 0)
 
         landing = keep.tile([P, PLANES], U8, align_bytes=64)
-        for first, scales in ((WA, wa_scales), (WC, wc_scales), (XT, xt_scales),
-                              (XQ, xq_scales), (WY, wy_scales), (WB, wb_scales)):
+
+        def load_scales(queue, scales, first):
             width = scales.shape[2]
-            nc.sync.dma_start(
+            queue.dma_start(
                 out=landing[4:P:8, first : first + width].bitcast(I32), in_=scales[0].bitcast(I32)
             )
-        wa_raw = load_words("wa_raw", wa_words[0], 2, 0, R)
-        wc_raw = load_words("wc_raw", wc_words[0], 2, 0, R)
-        for r in range(4):
-            nc.sync.dma_start(
-                out=planes[r:P:32, :].bitcast(I32), in_=landing[4 + 8 * r : P : 32, :].bitcast(I32)
-            )
-        xt_head = load_words("xt_head", xt_flat, 4, 0, CHUNK)
-        xq_head = load_words("xq_head", xq_flat, 4, 0, CHUNK)
-        xt_rest = load_words("xt_rest", xt_flat, 4, CHUNK, T)
-        xq_rest = load_words("xq_rest", xq_flat, 4, CHUNK, T)
-        wy = load_words("wy", wy_words[0], 2, 0, N)
-        wb = load_words("wb", wb_flat, 4, 0, N)
+
+        def spread_scales(first, last):
+            for r in range(4):
+                src = landing[4 + 8 * r : P : 32, :].bitcast(I32).rearrange("p (s w) -> p s w", s=2)
+                dst = planes[r:P:32, :].bitcast(I32).rearrange("p (s w) -> p s w", s=2)
+                nc.sync.dma_start(
+                    out=dst[:, :, first // 4 : last // 4], in_=src[:, :, first // 4 : last // 4]
+                )
+
+        load_scales(nc.sync, wa_scales, WA)
+        load_scales(nc.scalar, wc_scales, WC)
+        load_scales(nc.sync, xt_scales, XT)
+        load_scales(nc.scalar, xq_scales, XQ)
+        wa_raw = load_words(nc.sync, "wa_raw", wa_words[0], 2, 0, R)
+        wc_raw = load_words(nc.scalar, "wc_raw", wc_words[0], 2, 0, R)
+        xt_head = load_words(nc.sync, "xt_head", xt_flat, 4, 0, CHUNK)
+        xq_head = load_words(nc.scalar, "xq_head", xq_flat, 4, 0, CHUNK)
+        spread_scales(0, EARLY)
+        load_scales(nc.sync, wy_scales, WY)
+        load_scales(nc.sync, wb_scales, WB)
+        xt_rest = load_words(nc.sync, "xt_rest", xt_flat, 4, CHUNK, T)
+        xq_rest = load_words(nc.sync, "xq_rest", xq_flat, 4, CHUNK, T)
+        spread_scales(EARLY, SIDE)
+        wy = load_words(nc.sync, "wy", wy_words[0], 2, 0, N)
+        wb = load_words(nc.sync, "wb", wb_flat, 4, 0, N)
 
         def tokens(head, rest, first, count):
             if first < CHUNK:
@@ -86,10 +102,11 @@ def tile_mix_hidden_peaks_of_pairs_kernel(
                 in_=raw[:].bitcast(U16).rearrange("p (m j) -> p j m", j=PACK),
             )
             plane = keep.tile([P, R], U8, name=name + "_plane", align_bytes=64)
-            nc.vector.tensor_copy(
-                out=plane[:].rearrange("p (j m) -> p j m", j=PACK),
-                in_=planes[:, first : first + R].rearrange("p (m j) -> p j m", j=PACK),
-            )
+            for j in range(0, PACK, 2):
+                nc.vector.tensor_copy(
+                    out=plane[:].rearrange("p (j m) -> p j m", j=PACK)[:, j : j + 2, :],
+                    in_=planes[:, first : first + R].rearrange("p (m j) -> p j m", j=PACK)[:, j : j + 2, :],
+                )
             first_layer.append((words, plane))
         inputs = ((xt_head, xt_rest, XT), (xq_head, xq_rest, XQ))
 
@@ -129,7 +146,7 @@ def tile_mix_hidden_peaks_of_pairs_kernel(
             )
 
         def skip(c, h):
-            q = psum.tile([P, BANK], F32, name="q", tag="q%d" % (2 * (c % 2) + h))
+            q = psum.tile([P, BANK], F32, name="q", tag="q%d" % ((2 * c + h) % 3))
             for i in range(2):
                 rows = (2 * h + i) * P
                 nc.tensor.matmul_mx(
@@ -143,40 +160,48 @@ def tile_mix_hidden_peaks_of_pairs_kernel(
                 )
             skips[c, h] = q
 
+        def pieces(c):
+            count = 1 if c == CHUNKS - 1 else 2
+            return [(i, count) for i in range(0, N // P, count)]
+
         def second_layer(c):
-            p = psum.tile([P, BANK], F32, name="p", tag="p")
-            for i in range(N // P):
-                nc.tensor.matmul_mx(
-                    out=p[:, i * PAIRS : (i + 1) * PAIRS],
-                    lhsT=wb[:, 4 * i * P : 4 * (i + 1) * P].bitcast(FP8X4),
-                    lhsT_scale=planes[:, WB + i * P : WB + (i + 1) * P],
-                    rhs=codes[c][:].bitcast(FP8X4),
-                    rhs_scale=code_planes[c][:],
-                    start=True,
-                    stop=True,
-                )
             for h in range(2):
-                th = work.tile([P, 2, PAIRS], F32, name="th", tag="th%d" % h)
-                nc.scalar.activation(
-                    out=th[:].rearrange("p i b -> p (i b)"),
-                    in_=p[:, 2 * h * PAIRS : 2 * (h + 1) * PAIRS],
-                    func=mybir.ActivationFunctionType.Tanh,
-                )
-                squashed[c, h] = th
+                p = psum.tile([P, 2 * PAIRS], F32, name="p", tag="p%d" % h)
+                for i in range(2):
+                    rows = (2 * h + i) * P
+                    nc.tensor.matmul_mx(
+                        out=p[:, i * PAIRS : (i + 1) * PAIRS],
+                        lhsT=wb[:, 4 * rows : 4 * (rows + P)].bitcast(FP8X4),
+                        lhsT_scale=planes[:, WB + rows : WB + rows + P],
+                        rhs=codes[c][:].bitcast(FP8X4),
+                        rhs_scale=code_planes[c][:],
+                        start=True,
+                        stop=True,
+                    )
+                for i, count in pieces(c):
+                    if i // 2 == h:
+                        th = work.tile([P, count, PAIRS], F32, name="th", tag="th%d" % i)
+                        nc.scalar.activation(
+                            out=th[:].rearrange("p i b -> p (i b)"),
+                            in_=p[:, (i % 2) * PAIRS : (i % 2 + count) * PAIRS],
+                            func=mybir.ActivationFunctionType.Tanh,
+                        )
+                        squashed[c, i] = th
 
         out_rows = out.rearrange("(i p) t -> p i t", p=P)
 
         def finish(c):
-            for h in range(2):
-                y = work.tile([P, 2, CHUNK], F32, name="y", tag="y%d" % h)
+            for i, count in pieces(c):
+                y = work.tile([P, count, CHUNK], F32, name="y", tag="y%d" % i)
+                q = skips[c, i // 2][:, (i % 2) * CHUNK : (i % 2 + count) * CHUNK]
                 nc.vector.tensor_tensor(
                     out=y[:].rearrange("p i (b e) -> p i b e", e=2),
-                    in0=skips[c, h][:].rearrange("p (i b e) -> p i b e", i=2, e=2),
-                    in1=squashed[c, h][:].unsqueeze(3).to_broadcast([P, 2, PAIRS, 2]),
+                    in0=q.rearrange("p (i b e) -> p i b e", i=count, e=2),
+                    in1=squashed[c, i][:].unsqueeze(3).to_broadcast([P, count, PAIRS, 2]),
                     op=ALU.add,
                 )
                 nc.sync.dma_start(
-                    out=out_rows[:, 2 * h : 2 * h + 2, c * CHUNK : (c + 1) * CHUNK], in_=y[:]
+                    out=out_rows[:, i : i + count, c * CHUNK : (c + 1) * CHUNK], in_=y[:]
                 )
 
         def first_stage(c):

@@ -28,6 +28,7 @@ WA, XT, WY = 0, R, R + T
 WC, XQ, WB = SIDE + WA, SIDE + XT, SIDE + WY
 PLANES = 2 * SIDE
 EARLY = R + T // 2
+WARM_UPS = 5
 
 
 def tile_mix_hidden_peaks_of_pairs_kernel(
@@ -57,6 +58,7 @@ def tile_mix_hidden_peaks_of_pairs_kernel(
         nc.vector.memset(planes[:].bitcast(I32), 0)
 
         landing = keep.tile([P, PLANES], U8, align_bytes=64)
+        nc.gpsimd.memset(landing[:, WA : WA + CHUNK].bitcast(I32), 0)
 
         def load_scales(queue, scales, first):
             width = scales.shape[2]
@@ -93,6 +95,18 @@ def tile_mix_hidden_peaks_of_pairs_kernel(
             if first < CHUNK:
                 return head[:, 4 * first : 4 * (first + count)].bitcast(FP8X4)
             return rest[:, 4 * (first - CHUNK) : 4 * (first - CHUNK + count)].bitcast(FP8X4)
+
+        unread = psum.tile([P, 2 * PAIRS], F32, name="unread", tag="p0")
+        for n in range(WARM_UPS):
+            nc.tensor.matmul_mx(
+                out=unread[:],
+                lhsT=wa_raw[:, : 2 * P].bitcast(FP4X4),
+                lhsT_scale=landing[:, WA : WA + P],
+                rhs=tokens(xt_head, xt_rest, 0, CHUNK),
+                rhs_scale=landing[:, WA : WA + CHUNK],
+                start=True,
+                stop=True,
+            )
 
         first_layer = []
         for name, raw, first in (("wa", wa_raw, WA), ("wc", wc_raw, WC)):

@@ -29,6 +29,7 @@ WC, XQ, WB = SIDE + WA, SIDE + XT, SIDE + WY
 PLANES = 2 * SIDE
 EARLY = R + T // 2
 WARM_UPS = 5
+TOKEN_PIECES = ((0, CHUNK), (CHUNK, 5 * STRIP), (5 * STRIP, T))
 
 
 def tile_mix_hidden_peaks_of_pairs_kernel(
@@ -58,7 +59,7 @@ def tile_mix_hidden_peaks_of_pairs_kernel(
         nc.vector.memset(planes[:].bitcast(I32), 0)
 
         landing = keep.tile([P, PLANES], U8, align_bytes=64)
-        nc.gpsimd.memset(landing[:, WA : WA + CHUNK].bitcast(I32), 0)
+        nc.gpsimd.memset(landing[:, XQ : XQ + CHUNK].bitcast(I32), 0)
 
         def load_scales(queue, scales, first):
             width = scales.shape[2]
@@ -74,36 +75,52 @@ def tile_mix_hidden_peaks_of_pairs_kernel(
                     out=dst[:, :, first // 4 : last // 4], in_=src[:, :, first // 4 : last // 4]
                 )
 
+        xt = keep.tile([P, 4 * T], U8, align_bytes=64)
+        xq = keep.tile([P, 4 * T], U8, align_bytes=64)
+
+        def load_tokens(queue, tile, flat, piece):
+            first, last = TOKEN_PIECES[piece]
+            queue.dma_start(
+                out=tile[:, 4 * first : 4 * last].bitcast(I32),
+                in_=flat[:, 4 * first : 4 * last].bitcast(I32),
+            )
+
         load_scales(nc.sync, wa_scales, WA)
         load_scales(nc.scalar, wc_scales, WC)
         load_scales(nc.sync, xt_scales, XT)
         load_scales(nc.scalar, xq_scales, XQ)
         wa_raw = load_words(nc.sync, "wa_raw", wa_words[0], 2, 0, R)
         wc_raw = load_words(nc.scalar, "wc_raw", wc_words[0], 2, 0, R)
-        xt_head = load_words(nc.sync, "xt_head", xt_flat, 4, 0, CHUNK)
-        xq_head = load_words(nc.scalar, "xq_head", xq_flat, 4, 0, CHUNK)
+        load_tokens(nc.sync, xt, xt_flat, 0)
+        load_tokens(nc.scalar, xq, xq_flat, 0)
         spread_scales(0, EARLY)
         load_scales(nc.sync, wy_scales, WY)
         load_scales(nc.sync, wb_scales, WB)
-        xt_rest = load_words(nc.sync, "xt_rest", xt_flat, 4, CHUNK, T)
-        xq_rest = load_words(nc.sync, "xq_rest", xq_flat, 4, CHUNK, T)
+        load_tokens(nc.sync, xt, xt_flat, 1)
+        load_tokens(nc.sync, xq, xq_flat, 1)
         spread_scales(EARLY, SIDE)
         wy = load_words(nc.sync, "wy", wy_words[0], 2, 0, N)
         wb = load_words(nc.sync, "wb", wb_flat, 4, 0, N)
+        load_tokens(nc.sync, xt, xt_flat, 2)
+        load_tokens(nc.sync, xq, xq_flat, 2)
 
-        def tokens(head, rest, first, count):
-            if first < CHUNK:
-                return head[:, 4 * first : 4 * (first + count)].bitcast(FP8X4)
-            return rest[:, 4 * (first - CHUNK) : 4 * (first - CHUNK + count)].bitcast(FP8X4)
+        def tokens(tile, first, count):
+            return tile[:, 4 * first : 4 * (first + count)].bitcast(FP8X4)
+
+        def xt_plane(first, count):
+            return planes[:, XT + first : XT + first + count]
+
+        def xq_plane(first, count):
+            return planes[:, XQ + first : XQ + first + count]
 
         unread = psum.tile([P, 2 * PAIRS], F32, name="unread", tag="p0")
         for n in range(WARM_UPS):
             nc.tensor.matmul_mx(
                 out=unread[:],
                 lhsT=wa_raw[:, : 2 * P].bitcast(FP4X4),
-                lhsT_scale=landing[:, WA : WA + P],
-                rhs=tokens(xt_head, xt_rest, 0, CHUNK),
-                rhs_scale=landing[:, WA : WA + CHUNK],
+                lhsT_scale=landing[:, XQ : XQ + P],
+                rhs=tokens(xt, 0, CHUNK),
+                rhs_scale=landing[:, XQ : XQ + CHUNK],
                 start=True,
                 stop=True,
             )
@@ -122,7 +139,7 @@ def tile_mix_hidden_peaks_of_pairs_kernel(
                     in_=planes[:, first : first + R].rearrange("p (m j) -> p j m", j=PACK)[:, j : j + 2, :],
                 )
             first_layer.append((words, plane))
-        inputs = ((xt_head, xt_rest, XT), (xq_head, xq_rest, XQ))
+        inputs = ((xt, xt_plane), (xq, xq_plane))
 
         hidden, codes, code_planes, skips, squashed = {}, {}, {}, {}, {}
 
@@ -132,14 +149,14 @@ def tile_mix_hidden_peaks_of_pairs_kernel(
             z = psum.tile([P, BANK], F32, name="z", tag="z%d" % (strip % 3))
             for g in range(2):
                 words, plane = first_layer[g]
-                head, rest, x_plane = inputs[g]
+                x, x_plane = inputs[g]
                 for j in range(PACK):
                     nc.tensor.matmul_mx(
                         out=z[:, j * STRIP : (j + 1) * STRIP],
                         lhsT=words[:, 2 * j * P : 2 * (j + 1) * P].bitcast(FP4X4),
                         lhsT_scale=plane[:, j * P : (j + 1) * P],
-                        rhs=tokens(head, rest, first, STRIP),
-                        rhs_scale=planes[:, x_plane + first : x_plane + first + STRIP],
+                        rhs=tokens(x, first, STRIP),
+                        rhs_scale=x_plane(first, STRIP),
                         start=(g == 0 and j == 0),
                         stop=(g == 1 and j == PACK - 1),
                     )
@@ -167,8 +184,8 @@ def tile_mix_hidden_peaks_of_pairs_kernel(
                     out=q[:, i * CHUNK : (i + 1) * CHUNK],
                     lhsT=wy[:, 2 * rows : 2 * (rows + P)].bitcast(FP4X4),
                     lhsT_scale=planes[:, WY + rows : WY + rows + P],
-                    rhs=tokens(xt_head, xt_rest, c * CHUNK, CHUNK),
-                    rhs_scale=planes[:, XT + c * CHUNK : XT + (c + 1) * CHUNK],
+                    rhs=tokens(xt, c * CHUNK, CHUNK),
+                    rhs_scale=xt_plane(c * CHUNK, CHUNK),
                     start=True,
                     stop=True,
                 )
@@ -204,16 +221,26 @@ def tile_mix_hidden_peaks_of_pairs_kernel(
 
         out_rows = out.rearrange("(i p) t -> p i t", p=P)
 
+        def add_pairs(engine, y, q, th, count):
+            engine.tensor_tensor(
+                out=y.rearrange("p i (b e) -> p i b e", e=2),
+                in0=q.rearrange("p (i b e) -> p i b e", i=count, e=2),
+                in1=th.unsqueeze(3).to_broadcast([P, count, PAIRS, 2]),
+                op=ALU.add,
+            )
+
         def finish(c):
             for i, count in pieces(c):
                 y = work.tile([P, count, CHUNK], F32, name="y", tag="y%d" % i)
                 q = skips[c, i // 2][:, (i % 2) * CHUNK : (i % 2 + count) * CHUNK]
-                nc.vector.tensor_tensor(
-                    out=y[:].rearrange("p i (b e) -> p i b e", e=2),
-                    in0=q.rearrange("p (i b e) -> p i b e", i=count, e=2),
-                    in1=squashed[c, i][:].unsqueeze(3).to_broadcast([P, count, PAIRS, 2]),
-                    op=ALU.add,
-                )
+                th = squashed[c, i]
+                if i == 2 and count == 2:
+                    moved = work.tile([P, CHUNK], F32, name="moved")
+                    nc.scalar.copy(out=moved[:], in_=q[:, CHUNK:])
+                    add_pairs(nc.gpsimd, y[:, 1:2, :], moved[:], th[:, 1:2, :], 1)
+                    add_pairs(nc.vector, y[:, 0:1, :], q[:, :CHUNK], th[:, 0:1, :], 1)
+                else:
+                    add_pairs(nc.vector, y[:], q, th[:], count)
                 nc.sync.dma_start(
                     out=out_rows[:, i : i + count, c * CHUNK : (c + 1) * CHUNK], in_=y[:]
                 )

@@ -17,19 +17,41 @@ ALU = mybir.AluOpType
 
 P = 128
 PACK = 4
+FP8_BYTES, FP4_BYTES = 4, 2
 BANK = 512
 STRIP = 128
-CHUNK = 256
+CHUNK = 2 * STRIP
 PAIRS = CHUNK // 2
 CHUNKS = T // CHUNK
+LAST = CHUNKS - 1
+ROW_TILES = N // P
 
 SIDE = R + T + N
 WA, XT, WY = 0, R, R + T
 WC, XQ, WB = SIDE + WA, SIDE + XT, SIDE + WY
-PLANES = 2 * SIDE
 EARLY = R + T // 2
+
+TOKEN_LOADS = ((0, CHUNK), (CHUNK, 5 * STRIP), (5 * STRIP, T))
+
 WARM_UPS = 5
-TOKEN_PIECES = ((0, CHUNK), (CHUNK, 5 * STRIP), (5 * STRIP, T))
+SHARED_TILE = 3
+
+
+def strip_bank(strip):
+    if strip == 3:
+        return "skip2"
+    return "strip%d" % ((strip if strip < 3 else strip - 1) % 3)
+
+
+def skip_bank(c, h):
+    if (c, h) == (LAST, 1):
+        return strip_bank(5)
+    return "skip%d" % ((2 * c + h) % 3)
+
+
+def tanh_pieces(c):
+    count = 1 if c == LAST else 2
+    return [(i, count) for i in range(0, ROW_TILES, count)]
 
 
 def tile_mix_hidden_peaks_of_pairs_kernel(
@@ -43,22 +65,10 @@ def tile_mix_hidden_peaks_of_pairs_kernel(
         psum = ctx.enter_context(tc.psum_pool(name="psum", bufs=1))
         ctx.enter_context(tc.manual_schedule())
 
-        def load_words(queue, name, words, bytes_a_column, first, last):
-            tile = keep.tile([P, (last - first) * bytes_a_column], U8, name=name, align_bytes=64)
-            queue.dma_start(
-                out=tile[:].bitcast(I32),
-                in_=words[:, first * bytes_a_column : last * bytes_a_column].bitcast(I32),
-            )
-            return tile
-
-        xt_flat = xt_words[0].rearrange("p n t -> p (n t)")
-        xq_flat = xq_words[0].rearrange("p n t -> p (n t)")
-        wb_flat = wb_words[0].rearrange("p n t -> p (n t)")
-
-        planes = keep.tile([P, PLANES], U8, align_bytes=64)
+        planes = keep.tile([P, 2 * SIDE], U8, align_bytes=64)
         nc.vector.memset(planes[:].bitcast(I32), 0)
 
-        landing = keep.tile([P, PLANES], U8, align_bytes=64)
+        landing = keep.tile([P, 2 * SIDE], U8, align_bytes=64)
         nc.gpsimd.memset(landing[:, XQ : XQ + CHUNK].bitcast(I32), 0)
 
         def load_scales(queue, scales, first):
@@ -68,66 +78,72 @@ def tile_mix_hidden_peaks_of_pairs_kernel(
             )
 
         def spread_scales(first, last):
-            for r in range(4):
-                src = landing[4 + 8 * r : P : 32, :].bitcast(I32).rearrange("p (s w) -> p s w", s=2)
-                dst = planes[r:P:32, :].bitcast(I32).rearrange("p (s w) -> p s w", s=2)
+            for s in range(4):
+                src = landing[4 + 8 * s : P : 32, :].bitcast(I32).rearrange("p (side w) -> p side w", side=2)
+                dst = planes[s:P:32, :].bitcast(I32).rearrange("p (side w) -> p side w", side=2)
                 nc.sync.dma_start(
                     out=dst[:, :, first // 4 : last // 4], in_=src[:, :, first // 4 : last // 4]
                 )
 
-        xt = keep.tile([P, 4 * T], U8, align_bytes=64)
-        xq = keep.tile([P, 4 * T], U8, align_bytes=64)
+        def load_weight(queue, name, words):
+            tile = keep.tile([P, words.shape[1]], U8, name=name, align_bytes=64)
+            queue.dma_start(out=tile[:].bitcast(I32), in_=words.bitcast(I32))
+            return tile
 
-        def load_tokens(queue, tile, flat, piece):
-            first, last = TOKEN_PIECES[piece]
+        xt = keep.tile([P, FP8_BYTES * T], U8, align_bytes=64)
+        xq = keep.tile([P, FP8_BYTES * T], U8, align_bytes=64)
+
+        def load_tokens(queue, tile, words, part):
+            first, last = TOKEN_LOADS[part]
+            columns = slice(FP8_BYTES * first, FP8_BYTES * last)
             queue.dma_start(
-                out=tile[:, 4 * first : 4 * last].bitcast(I32),
-                in_=flat[:, 4 * first : 4 * last].bitcast(I32),
+                out=tile[:, columns].bitcast(I32),
+                in_=words[0].rearrange("p n t -> p (n t)")[:, columns].bitcast(I32),
             )
 
         load_scales(nc.sync, wa_scales, WA)
         load_scales(nc.scalar, wc_scales, WC)
         load_scales(nc.sync, xt_scales, XT)
         load_scales(nc.scalar, xq_scales, XQ)
-        wa_raw = load_words(nc.sync, "wa_raw", wa_words[0], 2, 0, R)
-        wc_raw = load_words(nc.scalar, "wc_raw", wc_words[0], 2, 0, R)
-        load_tokens(nc.sync, xt, xt_flat, 0)
-        load_tokens(nc.scalar, xq, xq_flat, 0)
+        wa_raw = load_weight(nc.sync, "wa_raw", wa_words[0])
+        wc_raw = load_weight(nc.scalar, "wc_raw", wc_words[0])
+        load_tokens(nc.sync, xt, xt_words, 0)
+        load_tokens(nc.scalar, xq, xq_words, 0)
         spread_scales(0, EARLY)
         load_scales(nc.sync, wy_scales, WY)
         load_scales(nc.sync, wb_scales, WB)
-        load_tokens(nc.sync, xt, xt_flat, 1)
-        load_tokens(nc.sync, xq, xq_flat, 1)
+        load_tokens(nc.sync, xt, xt_words, 1)
+        load_tokens(nc.sync, xq, xq_words, 1)
         spread_scales(EARLY, SIDE)
-        wy = load_words(nc.sync, "wy", wy_words[0], 2, 0, N)
-        wb = load_words(nc.sync, "wb", wb_flat, 4, 0, N)
-        load_tokens(nc.sync, xt, xt_flat, 2)
-        load_tokens(nc.sync, xq, xq_flat, 2)
+        wy = load_weight(nc.sync, "wy", wy_words[0])
+        wb = load_weight(nc.sync, "wb", wb_words[0].rearrange("p n t -> p (n t)"))
+        load_tokens(nc.sync, xt, xt_words, 2)
+        load_tokens(nc.sync, xq, xq_words, 2)
 
-        def tokens(tile, first, count):
-            return tile[:, 4 * first : 4 * (first + count)].bitcast(FP8X4)
+        def fp8(tile, first, count):
+            return tile[:, FP8_BYTES * first : FP8_BYTES * (first + count)].bitcast(FP8X4)
 
-        def xt_plane(first, count):
-            return planes[:, XT + first : XT + first + count]
+        def fp4(tile, first, count):
+            return tile[:, FP4_BYTES * first : FP4_BYTES * (first + count)].bitcast(FP4X4)
 
-        def xq_plane(first, count):
-            return planes[:, XQ + first : XQ + first + count]
+        def plane_of(operand, first, count):
+            return planes[:, operand + first : operand + first + count]
 
-        unread = psum.tile([P, 2 * PAIRS], F32, name="unread", tag="p0")
-        for n in range(WARM_UPS):
+        unread = psum.tile([P, CHUNK], F32, name="unread", tag="second0")
+        for repeat in range(WARM_UPS):
             nc.tensor.matmul_mx(
                 out=unread[:],
-                lhsT=wa_raw[:, : 2 * P].bitcast(FP4X4),
+                lhsT=fp4(wa_raw, 0, P),
                 lhsT_scale=landing[:, XQ : XQ + P],
-                rhs=tokens(xt, 0, CHUNK),
+                rhs=fp8(xt, 0, CHUNK),
                 rhs_scale=landing[:, XQ : XQ + CHUNK],
                 start=True,
                 stop=True,
             )
 
         first_layer = []
-        for name, raw, first in (("wa", wa_raw, WA), ("wc", wc_raw, WC)):
-            words = keep.tile([P, 2 * R], U8, name=name + "_words", align_bytes=64)
+        for name, raw, weight_plane, x, x_plane in (("wa", wa_raw, WA, xt, XT), ("wc", wc_raw, WC, xq, XQ)):
+            words = keep.tile([P, FP4_BYTES * R], U8, name=name + "_words", align_bytes=64)
             nc.scalar.copy(
                 out=words[:].bitcast(U16).rearrange("p (j m) -> p j m", j=PACK),
                 in_=raw[:].bitcast(U16).rearrange("p (m j) -> p j m", j=PACK),
@@ -136,125 +152,132 @@ def tile_mix_hidden_peaks_of_pairs_kernel(
             for j in range(0, PACK, 2):
                 nc.vector.tensor_copy(
                     out=plane[:].rearrange("p (j m) -> p j m", j=PACK)[:, j : j + 2, :],
-                    in_=planes[:, first : first + R].rearrange("p (m j) -> p j m", j=PACK)[:, j : j + 2, :],
+                    in_=plane_of(weight_plane, 0, R).rearrange("p (m j) -> p j m", j=PACK)[:, j : j + 2, :],
                 )
-            first_layer.append((words, plane))
-        inputs = ((xt, xt_plane), (xq, xq_plane))
+            first_layer.append((words, plane, x, x_plane))
 
-        hidden, codes, code_planes, skips, squashed = {}, {}, {}, {}, {}
+        z, hid, codes, code_plane, skip, tanh_p, skip_copy = {}, {}, {}, {}, {}, {}, {}
+
+        def hidden_passes(strip, product):
+            if product == 0:
+                z[strip] = psum.tile([P, BANK], F32, name="z", tag=strip_bank(strip))
+            words, plane, x, x_plane = first_layer[product]
+            for j in range(PACK):
+                nc.tensor.matmul_mx(
+                    out=z[strip][:, j * STRIP : (j + 1) * STRIP],
+                    lhsT=fp4(words, j * P, P),
+                    lhsT_scale=plane[:, j * P : (j + 1) * P],
+                    rhs=fp8(x, strip * STRIP, STRIP),
+                    rhs_scale=plane_of(x_plane, strip * STRIP, STRIP),
+                    start=(product == 0 and j == 0),
+                    stop=(product == 1 and j == PACK - 1),
+                )
 
         def peaks(c, s):
-            first = c * CHUNK + s * STRIP
-            strip = 2 * c + s
-            z = psum.tile([P, BANK], F32, name="z", tag="z%d" % (strip % 3))
-            for g in range(2):
-                words, plane = first_layer[g]
-                x, x_plane = inputs[g]
-                for j in range(PACK):
-                    nc.tensor.matmul_mx(
-                        out=z[:, j * STRIP : (j + 1) * STRIP],
-                        lhsT=words[:, 2 * j * P : 2 * (j + 1) * P].bitcast(FP4X4),
-                        lhsT_scale=plane[:, j * P : (j + 1) * P],
-                        rhs=tokens(x, first, STRIP),
-                        rhs_scale=x_plane(first, STRIP),
-                        start=(g == 0 and j == 0),
-                        stop=(g == 1 and j == PACK - 1),
-                    )
             if s == 0:
-                hidden[c] = work.tile([P, PAIRS * PACK], BF16, name="hidden", align_bytes=64)
+                hid[c] = work.tile([P, PAIRS * PACK], BF16, name="hid", align_bytes=64)
             half = PAIRS * PACK // 2
-            peak = hidden[c][:, s * half : (s + 1) * half].rearrange("p (b j) -> p b j", j=PACK)
-            pairs = z[:].rearrange("p (j b e) -> p b j e", j=PACK, e=2)
+            peak = hid[c][:, s * half : (s + 1) * half].rearrange("p (b j) -> p b j", j=PACK)
+            pairs = z[2 * c + s][:].rearrange("p (j b e) -> p b j e", j=PACK, e=2)
             odd = work.tile([P, STRIP // 2, PACK], F32, name="odd", tag="odd%d" % s)
             nc.scalar.copy(out=odd[:], in_=pairs[:, :, :, 1])
             nc.vector.tensor_tensor(out=peak, in0=pairs[:, :, :, 0], in1=odd[:], op=ALU.max)
 
-        def quantise(c):
+        def hidden_layer(c):
+            if c == 0:
+                for s in range(2):
+                    hidden_passes(s, 0)
+            for s in range(2):
+                if c > 0:
+                    hidden_passes(2 * c + s, 0)
+                hidden_passes(2 * c + s, 1)
+                peaks(c, s)
             codes[c] = work.tile([P, PAIRS], U32, name="codes", align_bytes=64)
-            code_planes[c] = work.tile([P, PAIRS], U8, name="code_plane", align_bytes=64)
-            nc.vector.quantize_mx(
-                out=codes[c][:].bitcast(FP8X4), scales=code_planes[c][:], in_=hidden[c][:]
-            )
+            code_plane[c] = work.tile([P, PAIRS], U8, name="code_plane", align_bytes=64)
+            nc.vector.quantize_mx(out=codes[c][:].bitcast(FP8X4), scales=code_plane[c][:], in_=hid[c][:])
 
-        def skip(c, h):
-            q = psum.tile([P, BANK], F32, name="q", tag="q%d" % ((2 * c + h) % 3))
-            for i in range(2):
-                rows = (2 * h + i) * P
-                nc.tensor.matmul_mx(
-                    out=q[:, i * CHUNK : (i + 1) * CHUNK],
-                    lhsT=wy[:, 2 * rows : 2 * (rows + P)].bitcast(FP4X4),
-                    lhsT_scale=planes[:, WY + rows : WY + rows + P],
-                    rhs=tokens(xt, c * CHUNK, CHUNK),
-                    rhs_scale=xt_plane(c * CHUNK, CHUNK),
-                    start=True,
-                    stop=True,
-                )
-            skips[c, h] = q
-
-        def pieces(c):
-            count = 1 if c == CHUNKS - 1 else 2
-            return [(i, count) for i in range(0, N // P, count)]
-
-        def second_layer(c):
+        def skip_products(c):
             for h in range(2):
-                p = psum.tile([P, 2 * PAIRS], F32, name="p", tag="p%d" % h)
+                skip[c, h] = psum.tile([P, BANK], F32, name="skip", tag=skip_bank(c, h))
                 for i in range(2):
-                    rows = (2 * h + i) * P
+                    row = (2 * h + i) * P
                     nc.tensor.matmul_mx(
-                        out=p[:, i * PAIRS : (i + 1) * PAIRS],
-                        lhsT=wb[:, 4 * rows : 4 * (rows + P)].bitcast(FP8X4),
-                        lhsT_scale=planes[:, WB + rows : WB + rows + P],
-                        rhs=codes[c][:].bitcast(FP8X4),
-                        rhs_scale=code_planes[c][:],
+                        out=skip[c, h][:, i * CHUNK : (i + 1) * CHUNK],
+                        lhsT=fp4(wy, row, P),
+                        lhsT_scale=plane_of(WY, row, P),
+                        rhs=fp8(xt, c * CHUNK, CHUNK),
+                        rhs_scale=plane_of(XT, c * CHUNK, CHUNK),
                         start=True,
                         stop=True,
                     )
-                for i, count in pieces(c):
+
+        def skip_of(c, i):
+            return skip[c, i // 2][:, (i % 2) * CHUNK : (i % 2 + 1) * CHUNK]
+
+        def second_layer(c):
+            for h in range(2):
+                p = psum.tile([P, 2 * PAIRS], F32, name="p", tag="second%d" % h)
+                for i in range(2):
+                    row = (2 * h + i) * P
+                    nc.tensor.matmul_mx(
+                        out=p[:, i * PAIRS : (i + 1) * PAIRS],
+                        lhsT=fp8(wb, row, P),
+                        lhsT_scale=plane_of(WB, row, P),
+                        rhs=codes[c][:].bitcast(FP8X4),
+                        rhs_scale=code_plane[c][:],
+                        start=True,
+                        stop=True,
+                    )
+                for i, count in tanh_pieces(c):
                     if i // 2 == h:
-                        th = work.tile([P, count, PAIRS], F32, name="th", tag="th%d" % i)
+                        tanh_p[c, i] = work.tile([P, count, PAIRS], F32, name="tanh_p", tag="tanh_p%d" % i)
                         nc.scalar.activation(
-                            out=th[:].rearrange("p i b -> p (i b)"),
+                            out=tanh_p[c, i][:].rearrange("p i b -> p (i b)"),
                             in_=p[:, (i % 2) * PAIRS : (i % 2 + count) * PAIRS],
                             func=mybir.ActivationFunctionType.Tanh,
                         )
-                        squashed[c, i] = th
 
-        out_rows = out.rearrange("(i p) t -> p i t", p=P)
-
-        def add_pairs(engine, y, q, th, count):
+        def add_pairs(engine, y, per_token, per_pair, count):
             engine.tensor_tensor(
                 out=y.rearrange("p i (b e) -> p i b e", e=2),
-                in0=q.rearrange("p (i b e) -> p i b e", i=count, e=2),
-                in1=th.unsqueeze(3).to_broadcast([P, count, PAIRS, 2]),
+                in0=per_token.rearrange("p (i b e) -> p i b e", i=count, e=2),
+                in1=per_pair.unsqueeze(3).to_broadcast([P, count, PAIRS, 2]),
                 op=ALU.add,
             )
 
+        out_rows = out.rearrange("(i p) t -> p i t", p=P)
+
+        def store(c, i, count, y):
+            nc.sync.dma_start(out=out_rows[:, i : i + count, c * CHUNK : (c + 1) * CHUNK], in_=y[:])
+
         def finish(c):
-            for i, count in pieces(c):
-                y = work.tile([P, count, CHUNK], F32, name="y", tag="y%d" % i)
-                q = skips[c, i // 2][:, (i % 2) * CHUNK : (i % 2 + count) * CHUNK]
-                th = squashed[c, i]
-                if i == 2 and count == 2:
-                    moved = work.tile([P, CHUNK], F32, name="moved")
-                    nc.scalar.copy(out=moved[:], in_=q[:, CHUNK:])
-                    add_pairs(nc.gpsimd, y[:, 1:2, :], moved[:], th[:, 1:2, :], 1)
-                    add_pairs(nc.vector, y[:, 0:1, :], q[:, :CHUNK], th[:, 0:1, :], 1)
+            skip_copy[c] = work.tile([P, CHUNK], F32, name="skip_copy")
+            nc.scalar.copy(out=skip_copy[c][:], in_=skip_of(c, SHARED_TILE))
+            for h in range(2):
+                y = work.tile([P, 2, CHUNK], F32, name="y", tag="y%d" % h)
+                both = tanh_p[c, 2 * h]
+                if h == SHARED_TILE // 2:
+                    add_pairs(nc.gpsimd, y[:, 1:2, :], skip_copy[c][:], both[:, 1:2, :], 1)
+                    add_pairs(nc.vector, y[:, 0:1, :], skip_of(c, 2 * h), both[:, 0:1, :], 1)
                 else:
-                    add_pairs(nc.vector, y[:], q, th[:], count)
-                nc.sync.dma_start(
-                    out=out_rows[:, i : i + count, c * CHUNK : (c + 1) * CHUNK], in_=y[:]
-                )
+                    add_pairs(nc.vector, y[:], skip[c, h][:], both[:], 2)
+                store(c, 2 * h, 2, y)
 
-        def first_stage(c):
-            peaks(c, 0)
-            peaks(c, 1)
-            quantise(c)
+        def finish_last():
+            for i in range(ROW_TILES):
+                y = work.tile([P, 1, CHUNK], F32, name="y", tag="y_last%d" % i)
+                add_pairs(nc.vector, y[:], skip_of(LAST, i), tanh_p[LAST, i][:], 1)
+                store(LAST, i, 1, y)
 
-        first_stage(0)
-        for c in range(CHUNKS):
-            if c + 1 < CHUNKS:
-                first_stage(c + 1)
-            skip(c, 0)
-            second_layer(c)
-            skip(c, 1)
+        hidden_layer(0)
+        for c in range(LAST):
+            hidden_layer(c + 1)
+            if c > 0:
+                second_layer(c)
+            skip_products(c)
+            if c == 0:
+                second_layer(c)
             finish(c)
+        skip_products(LAST)
+        second_layer(LAST)
+        finish_last()

from contextlib import ExitStack

import concourse.mybir as mybir

K, L, T, R, N, B = 512, 512, 1024, 512, 512, 512
FLOPS = 2 * (K * R * T + L * R * T + R * N * B + K * N * T)

F32 = mybir.dt.float32
BF16 = mybir.dt.bfloat16
I32 = mybir.dt.int32
U32 = mybir.dt.uint32
U16 = mybir.dt.uint16
U8 = mybir.dt.uint8
FP8X4 = mybir.dt.float8_e4m3fn_x4
FP4X4 = mybir.dt.float4_e2m1fn_x4
ALU = mybir.AluOpType

P = 128
PACK = 4
FP8_BYTES, FP4_BYTES = 4, 2
BANK = 512
STRIP = 128
CHUNK = 2 * STRIP
PAIRS = CHUNK // 2
CHUNKS = T // CHUNK
LAST = CHUNKS - 1
ROW_TILES = N // P

SIDE = R + T + N
WA, XT, WY = 0, R, R + T
WC, XQ, WB = SIDE + WA, SIDE + XT, SIDE + WY
EARLY = R + T // 2

TOKEN_LOADS = ((0, CHUNK), (CHUNK, 5 * STRIP), (5 * STRIP, T))

WARM_UPS = 5
SHARED_TILE = 3


def strip_bank(strip):
    if strip == 3:
        return "skip2"
    return "strip%d" % ((strip if strip < 3 else strip - 1) % 3)


def skip_bank(c, h):
    if (c, h) == (LAST, 1):
        return strip_bank(5)
    return "skip%d" % ((2 * c + h) % 3)


def tanh_pieces(c):
    count = 1 if c == LAST else 2
    return [(i, count) for i in range(0, ROW_TILES, count)]


def tile_mix_hidden_peaks_of_pairs_kernel(
    tc, xt_words, xt_scales, wa_words, wa_scales, xq_words, xq_scales,
    wc_words, wc_scales, wb_words, wb_scales, wy_words, wy_scales, out,
):
    nc = tc.nc
    with ExitStack() as ctx:
        keep = ctx.enter_context(tc.tile_pool(name="keep", bufs=1))
        work = ctx.enter_context(tc.tile_pool(name="work", bufs=CHUNKS))
        psum = ctx.enter_context(tc.psum_pool(name="psum", bufs=1))
        ctx.enter_context(tc.manual_schedule())

        planes = keep.tile([P, 2 * SIDE], U8, align_bytes=64)
        nc.vector.memset(planes[:].bitcast(I32), 0)

        landing = keep.tile([P, 2 * SIDE], U8, align_bytes=64)
        nc.gpsimd.memset(landing[:, XQ : XQ + CHUNK].bitcast(I32), 0)

        def load_scales(queue, scales, first):
            width = scales.shape[2]
            queue.dma_start(
                out=landing[4:P:8, first : first + width].bitcast(I32), in_=scales[0].bitcast(I32)
            )

        def spread_scales(first, last):
            for s in range(4):
                src = landing[4 + 8 * s : P : 32, :].bitcast(I32).rearrange("p (side w) -> p side w", side=2)
                dst = planes[s:P:32, :].bitcast(I32).rearrange("p (side w) -> p side w", side=2)
                nc.sync.dma_start(
                    out=dst[:, :, first // 4 : last // 4], in_=src[:, :, first // 4 : last // 4]
                )

        def load_weight(queue, name, words):
            tile = keep.tile([P, words.shape[1]], U8, name=name, align_bytes=64)
            queue.dma_start(out=tile[:].bitcast(I32), in_=words.bitcast(I32))
            return tile

        xt = keep.tile([P, FP8_BYTES * T], U8, align_bytes=64)
        xq = keep.tile([P, FP8_BYTES * T], U8, align_bytes=64)

        def load_tokens(queue, tile, words, part):
            first, last = TOKEN_LOADS[part]
            columns = slice(FP8_BYTES * first, FP8_BYTES * last)
            queue.dma_start(
                out=tile[:, columns].bitcast(I32),
                in_=words[0].rearrange("p n t -> p (n t)")[:, columns].bitcast(I32),
            )

        load_scales(nc.sync, wa_scales, WA)
        load_scales(nc.scalar, wc_scales, WC)
        load_scales(nc.sync, xt_scales, XT)
        load_scales(nc.scalar, xq_scales, XQ)
        wa_raw = load_weight(nc.sync, "wa_raw", wa_words[0])
        wc_raw = load_weight(nc.scalar, "wc_raw", wc_words[0])
        load_tokens(nc.sync, xt, xt_words, 0)
        load_tokens(nc.scalar, xq, xq_words, 0)
        spread_scales(0, EARLY)
        load_scales(nc.sync, wy_scales, WY)
        load_scales(nc.sync, wb_scales, WB)
        load_tokens(nc.sync, xt, xt_words, 1)
        load_tokens(nc.sync, xq, xq_words, 1)
        spread_scales(EARLY, SIDE)
        wy = load_weight(nc.sync, "wy", wy_words[0])
        wb = load_weight(nc.sync, "wb", wb_words[0].rearrange("p n t -> p (n t)"))
        load_tokens(nc.sync, xt, xt_words, 2)
        load_tokens(nc.sync, xq, xq_words, 2)

        def fp8(tile, first, count):
            return tile[:, FP8_BYTES * first : FP8_BYTES * (first + count)].bitcast(FP8X4)

        def fp4(tile, first, count):
            return tile[:, FP4_BYTES * first : FP4_BYTES * (first + count)].bitcast(FP4X4)

        def plane_of(operand, first, count):
            return planes[:, operand + first : operand + first + count]

        unread = psum.tile([P, CHUNK], F32, name="unread", tag="second0")
        for repeat in range(WARM_UPS):
            nc.tensor.matmul_mx(
                out=unread[:],
                lhsT=fp4(wa_raw, 0, P),
                lhsT_scale=landing[:, XQ : XQ + P],
                rhs=fp8(xt, 0, CHUNK),
                rhs_scale=landing[:, XQ : XQ + CHUNK],
                start=True,
                stop=True,
            )

        first_layer = []
        for name, raw, weight_plane, x, x_plane in (("wa", wa_raw, WA, xt, XT), ("wc", wc_raw, WC, xq, XQ)):
            words = keep.tile([P, FP4_BYTES * R], U8, name=name + "_words", align_bytes=64)
            nc.scalar.copy(
                out=words[:].bitcast(U16).rearrange("p (j m) -> p j m", j=PACK),
                in_=raw[:].bitcast(U16).rearrange("p (m j) -> p j m", j=PACK),
            )
            plane = keep.tile([P, R], U8, name=name + "_plane", align_bytes=64)
            for j in range(0, PACK, 2):
                nc.vector.tensor_copy(
                    out=plane[:].rearrange("p (j m) -> p j m", j=PACK)[:, j : j + 2, :],
                    in_=plane_of(weight_plane, 0, R).rearrange("p (m j) -> p j m", j=PACK)[:, j : j + 2, :],
                )
            first_layer.append((words, plane, x, x_plane))

        z, hid, codes, code_plane, skip, tanh_p, skip_copy = {}, {}, {}, {}, {}, {}, {}

        def hidden_passes(strip, product):
            if product == 0:
                z[strip] = psum.tile([P, BANK], F32, name="z", tag=strip_bank(strip))
            words, plane, x, x_plane = first_layer[product]
            for j in range(PACK):
                nc.tensor.matmul_mx(
                    out=z[strip][:, j * STRIP : (j + 1) * STRIP],
                    lhsT=fp4(words, j * P, P),
                    lhsT_scale=plane[:, j * P : (j + 1) * P],
                    rhs=fp8(x, strip * STRIP, STRIP),
                    rhs_scale=plane_of(x_plane, strip * STRIP, STRIP),
                    start=(product == 0 and j == 0),
                    stop=(product == 1 and j == PACK - 1),
                )

        def peaks(c, s):
            if s == 0:
                hid[c] = work.tile([P, PAIRS * PACK], BF16, name="hid", align_bytes=64)
            half = PAIRS * PACK // 2
            peak = hid[c][:, s * half : (s + 1) * half].rearrange("p (b j) -> p b j", j=PACK)
            pairs = z[2 * c + s][:].rearrange("p (j b e) -> p b j e", j=PACK, e=2)
            odd = work.tile([P, STRIP // 2, PACK], F32, name="odd", tag="odd%d" % s)
            nc.scalar.copy(out=odd[:], in_=pairs[:, :, :, 1])
            nc.vector.tensor_tensor(out=peak, in0=pairs[:, :, :, 0], in1=odd[:], op=ALU.max)

        def hidden_layer(c):
            if c == 0:
                for s in range(2):
                    hidden_passes(s, 0)
            for s in range(2):
                if c > 0:
                    hidden_passes(2 * c + s, 0)
                hidden_passes(2 * c + s, 1)
                peaks(c, s)
            codes[c] = work.tile([P, PAIRS], U32, name="codes", align_bytes=64)
            code_plane[c] = work.tile([P, PAIRS], U8, name="code_plane", align_bytes=64)
            nc.vector.quantize_mx(out=codes[c][:].bitcast(FP8X4), scales=code_plane[c][:], in_=hid[c][:])

        def skip_products(c):
            for h in range(2):
                skip[c, h] = psum.tile([P, BANK], F32, name="skip", tag=skip_bank(c, h))
                for i in range(2):
                    row = (2 * h + i) * P
                    nc.tensor.matmul_mx(
                        out=skip[c, h][:, i * CHUNK : (i + 1) * CHUNK],
                        lhsT=fp4(wy, row, P),
                        lhsT_scale=plane_of(WY, row, P),
                        rhs=fp8(xt, c * CHUNK, CHUNK),
                        rhs_scale=plane_of(XT, c * CHUNK, CHUNK),
                        start=True,
                        stop=True,
                    )

        def skip_of(c, i):
            return skip[c, i // 2][:, (i % 2) * CHUNK : (i % 2 + 1) * CHUNK]

        def second_layer(c):
            for h in range(2):
                p = psum.tile([P, 2 * PAIRS], F32, name="p", tag="second%d" % h)
                for i in range(2):
                    row = (2 * h + i) * P
                    nc.tensor.matmul_mx(
                        out=p[:, i * PAIRS : (i + 1) * PAIRS],
                        lhsT=fp8(wb, row, P),
                        lhsT_scale=plane_of(WB, row, P),
                        rhs=codes[c][:].bitcast(FP8X4),
                        rhs_scale=code_plane[c][:],
                        start=True,
                        stop=True,
                    )
                for i, count in tanh_pieces(c):
                    if i // 2 == h:
                        tanh_p[c, i] = work.tile([P, count, PAIRS], F32, name="tanh_p", tag="tanh_p%d" % i)
                        nc.scalar.activation(
                            out=tanh_p[c, i][:].rearrange("p i b -> p (i b)"),
                            in_=p[:, (i % 2) * PAIRS : (i % 2 + count) * PAIRS],
                            func=mybir.ActivationFunctionType.Tanh,
                        )

        def add_pairs(engine, y, per_token, per_pair, count):
            engine.tensor_tensor(
                out=y.rearrange("p i (b e) -> p i b e", e=2),
                in0=per_token.rearrange("p (i b e) -> p i b e", i=count, e=2),
                in1=per_pair.unsqueeze(3).to_broadcast([P, count, PAIRS, 2]),
                op=ALU.add,
            )

        out_rows = out.rearrange("(i p) t -> p i t", p=P)

        def store(c, i, count, y):
            nc.sync.dma_start(out=out_rows[:, i : i + count, c * CHUNK : (c + 1) * CHUNK], in_=y[:])

        def finish(c):
            skip_copy[c] = work.tile([P, CHUNK], F32, name="skip_copy")
            nc.scalar.copy(out=skip_copy[c][:], in_=skip_of(c, SHARED_TILE))
            for h in range(2):
                y = work.tile([P, 2, CHUNK], F32, name="y", tag="y%d" % h)
                both = tanh_p[c, 2 * h]
                if h == SHARED_TILE // 2:
                    add_pairs(nc.gpsimd, y[:, 1:2, :], skip_copy[c][:], both[:, 1:2, :], 1)
                    add_pairs(nc.vector, y[:, 0:1, :], skip_of(c, 2 * h), both[:, 0:1, :], 1)
                else:
                    add_pairs(nc.vector, y[:], skip[c, h][:], both[:], 2)
                store(c, 2 * h, 2, y)

        def finish_last():
            for i in range(ROW_TILES):
                y = work.tile([P, 1, CHUNK], F32, name="y", tag="y_last%d" % i)
                add_pairs(nc.vector, y[:], skip_of(LAST, i), tanh_p[LAST, i][:], 1)
                store(LAST, i, 1, y)

        hidden_layer(0)
        for c in range(LAST):
            hidden_layer(c + 1)
            if c > 0:
                second_layer(c)
            skip_products(c)
            if c == 0:
                second_layer(c)
            finish(c)
        skip_products(LAST)
        second_layer(LAST)
        finish_last()
